import numpy as np
import ml_dtypes


def mxq(x, axis, fmt="e4m3"):
    dtype, down = {"e4m3": (ml_dtypes.float8_e4m3fn, 7), "e5m2": (ml_dtypes.float8_e5m2, 14)}[fmt]
    v = np.moveaxis(np.asarray(x, np.float32).astype(ml_dtypes.bfloat16).astype(np.float64), axis, -1)
    blocks = v.reshape(v.shape[:-1] + (-1, 32))
    amax = np.abs(blocks).max(-1, keepdims=True)
    byte = np.maximum(np.where(amax > 0, np.frexp(amax)[1] - 1 + 127, 0) - down, 1)
    scale = np.exp2(byte - 127.0)
    codes = (blocks / scale).astype(np.float32).astype(dtype).astype(np.float64)
    return np.moveaxis((codes * scale).reshape(v.shape), -1, axis)


WIDE = False


def mx_kscale(k):
    if not WIDE:
        return np.ones(k)
    levels = np.array([10, -10, 5, -5, 0])
    if k % 512:
        return np.exp2(np.random.permutation(np.resize(levels, k // 32))).repeat(32)
    a = np.empty((k // 512, 16))
    for p in range(k // 512):
        a[p, :8] = np.random.permutation(np.resize(levels, 8))
        for g in range(8):
            far = levels[np.abs(levels - a[p, g]) >= 10]
            a[p, g + 8] = far[np.random.randint(len(far))]
    return np.exp2(a.ravel()).repeat(32)


def f64(x):
    return np.asarray(x).astype(np.float64)


def striped(idx):
    return np.tile(idx.reshape(-1, 16).T, (8, 1)).astype(np.uint16)


def unstriped(offs):
    return offs[:16].T.reshape(-1).astype(np.int64)


E2M1 = np.array([0.0, 0.5, 1.0, 1.5, 2.0, 3.0, 4.0, 6.0, -0.0, -0.5, -1.0, -1.5, -2.0, -3.0, -4.0, -6.0])


def pack_weight(w, fmt):
    k, n = w.shape
    w = f64(np.asarray(w, np.float32).astype(ml_dtypes.bfloat16)).reshape(k // 32, 32, n)
    amax = np.abs(w).max(1)
    if fmt == "e4m3":
        byte = np.frexp(amax)[1] - 1 + 127 - 7
    else:
        mant, ex = np.frexp(amax / 6.0)
        byte = np.where(mant > 0.5, ex, ex - 1) + 127
    byte = np.clip(np.where(amax > 0, byte, 1), 1, 254)
    scaled = (w * np.exp2(127.0 - byte)[:, None, :]).reshape(k, n).astype(np.float32)
    by_word = np.ascontiguousarray(scaled.reshape(k // 512, 128, 4, n).transpose(0, 1, 3, 2))
    if fmt == "e4m3":
        words = by_word.astype(ml_dtypes.float8_e4m3fn).view(np.uint8)
    else:
        c = by_word.astype(ml_dtypes.float4_e2m1fn).view(np.uint8) & 0xF
        words = (c[..., 0::2] | (c[..., 1::2] << 4)).reshape(k // 512, 128, 2 * n)
    return np.ascontiguousarray(words), np.ascontiguousarray(byte.astype(np.uint8).reshape(k // 512, 16, n))


def unpack_weight(words, scales, fmt):
    g, _, n = scales.shape
    words = np.ascontiguousarray(words).reshape(g, 128, n, -1)
    if fmt == "e4m3":
        vals = words.view(ml_dtypes.float8_e4m3fn).astype(np.float64)
    else:
        nib = np.empty((g, 128, n, 4), np.uint8)
        nib[..., 0::2] = words & 0xF
        nib[..., 1::2] = words >> 4
        vals = E2M1[nib]
    vals = vals * np.repeat(np.exp2(scales.astype(np.float64) - 127.0), 8, axis=1)[..., None]
    return vals.transpose(0, 1, 3, 2).reshape(g * 512, n)


def gelu(v):
    return 0.5 * v * (1.0 + np.tanh(np.sqrt(2.0 / np.pi) * (v + 0.044715 * v**3)))


def bf(x):
    return np.asarray(x, np.float32).astype(ml_dtypes.bfloat16)


def planes(Y):
    n, m = Y.shape
    b = f64(bf(Y)).reshape(n // 32, 32, m)
    amax = np.abs(b).max(1)
    byte = np.clip(np.where(amax > 0, np.frexp(amax)[1] - 1 + 127 - 7, 1), 1, 254)
    codes = (b * np.exp2(127.0 - byte)[:, None, :]).reshape(n, m).astype(np.float32).astype(ml_dtypes.float8_e4m3fn).view(np.uint8)
    words = codes.reshape(n // 512, 128, 4, m).transpose(0, 1, 3, 2)
    return np.ascontiguousarray(words), np.ascontiguousarray(byte.astype(np.uint8).reshape(n // 512, 16, m))


K, T, S, H, T2, P, N = 1024, 2048, 1024, 1024, 2048, 512, 512


def setup_inputs():
    n = np.random.standard_normal
    s = mx_kscale(K)[:, None]
    u = mx_kscale(H)[:, None]
    d = {}
    d["tab_words"], d["tab_scales"] = pack_weight(n((K, T)) * s, "e4m3")
    d["offs"] = striped(np.random.permutation(T)[:S])
    d["offs2"] = striped(np.random.permutation(T2)[:S])
    d["offs3"] = striped(np.random.permutation(T2)[:P])
    d["w1"] = (n((K, H)) / s * u.T / K ** 0.5).astype(np.float32)
    d["w4_words"], d["w4_scales"] = pack_weight(n((K, H)) / s * u.T / K ** 0.5, "e2m1")
    d["wgs"] = np.exp(0.3 * n((128, S))).astype(np.float32)
    d["page0"] = (n((H, T2)) * u).astype(np.float32)
    d["swell"] = (n((H, P)) * u).astype(np.float32)
    d["w2"] = (0.7 * n((H, N)) / u / H ** 0.5).astype(np.float32)
    return d


def reference(tab_words, tab_scales, offs, offs2, offs3, w1, w4_words, w4_scales, wgs, page0, swell, w2):
    v = unpack_weight(tab_words, tab_scales, "e4m3")[:, unstriped(offs)]
    w4 = unpack_weight(w4_words, w4_scales, "e2m1")
    a = np.abs(mxq(f64(w1), 0, "e4m3").T @ v)
    b = np.abs(w4.T @ v)
    h = a + b
    page = f64(page0).copy()
    page[:, unstriped(offs2)] = np.tile(f64(wgs), (H // 128, 1)) * h
    x = page[:, unstriped(offs3)] + f64(swell)
    z = mxq(f64(w2), 0, "e4m3").T @ mxq(x, 0, "e4m3")
    y = np.exp(-np.abs(z))
    words, scales = planes(page)
    return y, page, words, scales

@@ -1,0 +1,337 @@
+from contextlib import ExitStack
+
+import concourse.mybir as mybir
+from concourse.masks import make_identity
+
+K, T, S, H, T2, M, N = 1024, 2048, 1024, 1024, 2048, 512, 512
+FLOPS = 2 * (2 * K * H * S + H * N * M)
+
+F32 = mybir.dt.float32
+BF16 = mybir.dt.bfloat16
+I32 = mybir.dt.int32
+U32 = mybir.dt.uint32
+U16 = mybir.dt.uint16
+U8 = mybir.dt.uint8
+FP8X4 = mybir.dt.float8_e4m3fn_x4
+FP4X4 = mybir.dt.float4_e2m1fn_x4
+ALU = mybir.AluOpType
+ACT = mybir.ActivationFunctionType
+
+P = 128
+PACK = 4
+PASS = P * PACK
+BANK = 512
+PER_COL = 16
+
+
+def tile_list_heat_slot_marks_kernel(
+    tc, tab_words, tab_scales, offs, offs2, offs3, w1, w4_words, w4_scales, wgs, page0, swell, w2,
+    out_0, out_1, out_2, out_3,
+):
+    nc = tc.nc
+    with ExitStack() as ctx:
+        lists = ctx.enter_context(tc.tile_pool(name="lists", bufs=1))
+        sb = ctx.enter_context(tc.tile_pool(name="sb", bufs=1))
+        ps = ctx.enter_context(tc.psum_pool(name="ps", bufs=1))
+
+        def entries(tile, first, count):
+            return tile[:, first // PER_COL : (first + count) // PER_COL]
+
+        def rows_by_four(matrix, g):
+            return matrix[PASS * g : PASS * (g + 1), :].rearrange("(p t) c -> p t c", t=PACK)
+
+        def page_rows(matrix, g, t):
+            return matrix[PASS * g + t : PASS * (g + 1) : PACK, :]
+
+        def load_scale_rows(plane, scales):
+            for q in range(4):
+                nc.sync.dma_start(
+                    out=plane[32 * q : 32 * q + 4, :, :].bitcast(I32),
+                    in_=scales[:, 4 * q : 4 * q + 4, :].rearrange("a r c -> r a c").bitcast(I32),
+                )
+
+        def interleave(copy, out, planes):
+            copy(
+                out=out.rearrange("p (c i t) -> p c t i", i=4, t=PACK),
+                in_=planes.rearrange("p t (c i) -> p c t i", i=4),
+            )
+
+        def quantise_raw(raw, codes, scales, copy, tag="grouped", bufs=3):
+            grouped = sb.tile([P, PACK * BANK], BF16, tag=tag, bufs=bufs, align_bytes=64, name="grouped")
+            interleave(copy, grouped[:], raw[:])
+            nc.vector.quantize_mx(out=codes[:].bitcast(FP8X4), scales=scales[:], in_=grouped[:])
+
+        def load_raw(source, tag):
+            raw = sb.tile([P, PACK, BANK], F32, tag=tag, align_bytes=64, name="raw")
+            nc.sync.dma_start(out=raw[:], in_=source)
+            return raw
+
+        def mx_tiles(name):
+            codes = sb.tile([P, BANK], U32, align_bytes=64, name=name + "_codes")
+            scales = sb.tile([P, BANK], U8, align_bytes=64, name=name + "_scales")
+            return codes, scales
+
+        def w1_source(a, g):
+            return w1[PASS * a : PASS * (a + 1), PASS * g : PASS * (g + 1)].rearrange("(p i) c -> p i c", i=PACK)
+
+        def load_page(g, t, tag, queue=nc.sync):
+            page = sb.tile([P, T2], F32, tag=tag, align_bytes=64, name="page")
+            queue.dma_start(out=page[:], in_=page_rows(page0, g, t))
+            return page
+
+        def load_table(a):
+            words = sb.tile([P, T], I32, tag="AB"[a], align_bytes=64, name="table")
+            nc.sync.dma_start(out=words[:], in_=tab_words[a].rearrange("p t i -> p (t i)").bitcast(I32))
+            return words
+
+        def load_w4(g):
+            words = sb.tile([P, 2, 2 * PASS], U8, align_bytes=64, tag="w4_words%d" % g, bufs=1, name="w4_words")
+            nc.sync.dma_start(
+                out=words[:].bitcast(I32),
+                in_=w4_words[:, :, 2 * PASS * g : 2 * PASS * (g + 1)].rearrange("a p c -> p a c").bitcast(I32),
+            )
+            return words
+
+        def load_gains(t):
+            gains = sb.tile([P, S], F32, tag="gains%d" % t, align_bytes=64, name="gains")
+            for rep in (0, 2, 1, 3):
+                nc.sync.dma_start(out=gains[32 * rep : 32 * rep + 32, :], in_=wgs[t:P:PACK, :])
+            return gains
+
+        idx = lists.tile([P, S // PER_COL], U16, name="idx")
+        idx2 = lists.tile([P, S // PER_COL], U16, name="idx2")
+        idx3 = lists.tile([P, M // PER_COL], U16, name="idx3")
+        table_scales = sb.tile([P, 2, T], U8, align_bytes=64, name="table_scales")
+        w4_plane = sb.tile([P, 2, H], U8, align_bytes=64, name="w4_plane")
+        nc.gpsimd.memset(table_scales[:, 0, :].bitcast(I32), 0)
+        nc.vector.memset(table_scales[:, 1, :].bitcast(I32), 0)
+        nc.vector.memset(w4_plane[:].rearrange("p a c -> p (a c)").bitcast(I32), 0)
+        warm = sb.tile([P, 2], F32, name="warm")
+        nc.vector.memset(warm[:, 0:1], 0.0)
+        nc.scalar.activation(out=warm[:, 1:2], in_=warm[:, 0:1], func=ACT.Exp)
+        ident = sb.tile([P, P], F32, tag="ident", align_bytes=64, name="ident")
+        make_identity(nc, ident[:])
+
+        nc.sync.dma_start(idx[:], offs)
+        table = [load_table(0)]
+        w1_raw = {(0, 0): load_raw(w1_source(0, 0), "E")}
+        load_scale_rows(table_scales, tab_scales)
+        w4 = [load_w4(0)]
+        nc.sync.dma_start(idx2[:], offs2)
+        w1_raw[1, 0] = load_raw(w1_source(1, 0), "F")
+        table.append(load_table(1))
+        load_scale_rows(w4_plane, w4_scales)
+        pages = {}
+        gains = []
+        for t in range(3):
+            pages[0, t] = load_page(0, t, "page0%d" % t)
+            gains.append(load_gains(t))
+
+        clip_words = [sb.tile([P, S], U32, tag="CD"[a], align_bytes=64, name="clip_words") for a in range(2)]
+        clip_scales = []
+
+        def gather_scales(tag):
+            first = len(clip_scales) * BANK
+            picked = sb.tile([P, 2, BANK], U8, tag=tag, align_bytes=64, name="clip_scales")
+            for a in range(2):
+                nc.vector.tensor_copy(picked[:, a, :], table_scales[:, a, :].indirect(entries(idx, first, BANK)))
+            clip_scales.append(picked)
+
+        def gather_words(a, first, count):
+            nc.vector.tensor_copy(
+                clip_words[a][:, first : first + count],
+                table[a][:].bitcast(U32).indirect(entries(idx, first, count)),
+            )
+
+        w1_mx = {}
+
+        def quantise_w1(a, g, *slot):
+            w1_mx[a, g] = mx_tiles("w1_%d%d" % (a, g))
+            quantise_raw(w1_raw[a, g], *w1_mx[a, g], nc.scalar.copy, *slot)
+
+        gather_words(0, 0, S)
+        gather_scales("early_scales")
+        quantise_w1(0, 0)
+        gather_words(1, 0, S // 4)
+        w1_mx[1, 0] = mx_tiles("w1_10")
+        grouped = sb.tile([P, PACK * BANK], BF16, tag="late_scales", align_bytes=64, name="grouped")
+        for half, copy in enumerate((nc.scalar.copy, nc.vector.tensor_copy)):
+            interleave(copy, grouped[:, 1024 * half : 1024 * (half + 1)], w1_raw[1, 0][:, :, 256 * half : 256 * (half + 1)])
+        nc.vector.quantize_mx(out=w1_mx[1, 0][0][:].bitcast(FP8X4), scales=w1_mx[1, 0][1][:], in_=grouped[:])
+        gather_words(1, S // 4, S // 4)
+        gather_scales("late_scales")
+        gather_words(1, S // 2, S // 2)
+
+        for a in range(2):
+            w1_raw[a, 1] = load_raw(w1_source(a, 1), "EF"[a])
+        w4.append(load_w4(1))
+        gains.append(load_gains(3))
+        nc.sync.dma_start(idx3[:], offs3)
+        swell_rows = {}
+
+        def load_swell(g, tag):
+            swell_rows[g] = sb.tile([P, PACK, M], F32, tag=tag, align_bytes=64, name="swell_rows")
+            nc.sync.dma_start(out=swell_rows[g][:], in_=rows_by_four(swell, g))
+
+        def make_h(g):
+            h = sb.tile([P, PACK, S], F32, tag="h%d" % g, align_bytes=64, name="h")
+            for jb in range(S // P):
+                cols = slice(P * jb, P * (jb + 1))
+                sizes = []
+                for second in range(2):
+                    bank = ps.tile([P, BANK], F32, tag="mm", bufs=4, name="reading")
+                    for a in range(2):
+                        if second:
+                            rhs = w4[g][:, a, :].bitcast(FP4X4)
+                            rhs_scale = w4_plane[:, a, PASS * g : PASS * (g + 1)]
+                        else:
+                            rhs = w1_mx[a, g][0][:].bitcast(FP8X4)
+                            rhs_scale = w1_mx[a, g][1][:]
+                        nc.tensor.matmul_mx(
+                            out=bank[:], lhsT=clip_words[a][:, cols].bitcast(FP8X4), lhsT_scale=clip_scales[jb // 4][:, a, P * (jb % 4) : P * (jb % 4 + 1)],
+                            rhs=rhs, rhs_scale=rhs_scale, start=(a == 0), stop=(a == 1),
+                        )
+                    size = sb.tile([P, PACK, P], F32, tag="staged", bufs=4, name="size")
+                    nc.scalar.activation(out=size[:], in_=bank[:].rearrange("j (q t) -> j t q", t=PACK), func=ACT.Abs)
+                    sizes.append(size)
+                if jb % 2 == 0:
+                    turned = [ps.tile([P, 2, 2 * P], F32, tag="turned", bufs=4, name="turned") for u in range(2)]
+                for t in range(PACK):
+                    for second in (1, 0):
+                        nc.tensor.matmul(
+                            out=turned[t // 2][:, t % 2, P * (jb % 2) : P * (jb % 2 + 1)], lhsT=sizes[second][:, t, :], rhs=ident[:],
+                            start=(second == 1), stop=(second == 0), is_transpose=True,
+                        )
+                    if jb % 2 == 1 and t % 2 == 1:
+                        nc.scalar.copy(out=h[:, t - 1 : t + 1, P * (jb - 1) : P * (jb + 1)], in_=turned[t // 2][:])
+            return h
+
+        def scatter(g, t, h, first, count):
+            nc.vector.tensor_tensor(
+                pages[g, t][:].indirect(entries(idx2, first, count)),
+                h[:, t, first : first + count], gains[t][:, first : first + count], ALU.mult,
+            )
+
+        def fetch(g, t, x):
+            nc.vector.tensor_tensor(x[:, t, :], pages[g, t][:].indirect(idx3[:]), swell_rows[g][:, t, :], ALU.add)
+
+        def store_page(g, t):
+            nc.sync.dma_start(out=page_rows(out_1, g, t), in_=pages[g, t][:])
+
+        def cast_plane(g, t, planes):
+            for half in range(2):
+                nc.scalar.copy(out=planes[half][:, t, :], in_=pages[g, t][:, S * half : S * (half + 1)])
+
+        def quantise_page(g, half, grouped, codes):
+            cols = slice(S * half, S * (half + 1))
+            nc.vector.quantize_mx(out=codes[:, cols].bitcast(FP8X4), scales=page_scales[:, g, cols], in_=grouped)
+
+        def store_codes(g, cols, codes):
+            nc.sync.dma_start(
+                out=out_2[g].rearrange("p m t -> p (m t)").bitcast(I32)[:, cols], in_=codes[:, cols].bitcast(I32)
+            )
+
+        page_scales = sb.tile([P, 2, T2], U8, align_bytes=64, name="page_scales")
+        h0 = make_h(0)
+        for q in range(4):
+            for t in range(3):
+                scatter(0, t, h0, 256 * q, 256)
+        quantise_w1(0, 1)
+        quantise_w1(1, 1)
+        pages[0, 3] = load_page(0, 3, "E")
+        load_swell(0, "F")
+        pages[1, 0] = load_page(1, 0, "page10")
+        pages[1, 1] = load_page(1, 1, "page11")
+        pages[1, 2] = load_page(1, 2, "page12")
+        w2_raw = [load_raw(rows_by_four(w2, g), "AB"[g]) for g in range(2)]
+        pages[1, 3] = load_page(1, 3, "page13")
+        h1 = make_h(1)
+        scatter(0, 3, h0, 0, S)
+        x0 = sb.tile([P, PACK, M], F32, tag="h0", align_bytes=64, name="x0")
+        for t in range(4):
+            fetch(0, t, x0)
+            store_page(0, t)
+        w2_mx = [mx_tiles("w2_%d" % g) for g in range(2)]
+        x_mx = [mx_tiles("x_%d" % g) for g in range(2)]
+        for g in range(2):
+            quantise_raw(w2_raw[g], *w2_mx[g], nc.scalar.copy)
+        load_swell(1, "A")
+        stage0 = [sb.tile([P, PACK, S], BF16, tag="CD"[half], align_bytes=64, name="stage0") for half in range(2)]
+        quantise_raw(x0, *x_mx[0], nc.scalar.copy, "ident", 1)
+        for t in range(4):
+            cast_plane(0, t, stage0)
+        scatter(1, 0, h1, 0, 512)
+        scatter(1, 0, h1, 512, 512)
+        for t in range(1, 4):
+            scatter(1, t, h1, 0, S)
+        grouped0 = sb.tile([P, PACK * T2], BF16, tag="h0", align_bytes=64, name="grouped0")
+        for half in range(2):
+            interleave(nc.scalar.copy, grouped0[:, PACK * S * half : PACK * S * (half + 1)], stage0[half][:])
+
+        HM = M // 2
+        marks = [[ps.tile([P, 2, HM], F32, tag="mm", bufs=4, name="marks") for u in range(2)] for hm in range(2)]
+
+        def marks_pass(g, hm):
+            for nb in range(N // P):
+                cols = slice(P * nb, P * (nb + 1))
+                slots = slice(HM * hm, HM * (hm + 1))
+                nc.tensor.matmul_mx(
+                    out=marks[hm][nb // 2][:, nb % 2, :], lhsT=w2_mx[g][0][:, cols].bitcast(FP8X4), lhsT_scale=w2_mx[g][1][:, cols],
+                    rhs=x_mx[g][0][:, slots].bitcast(FP8X4), rhs_scale=x_mx[g][1][:, slots],
+                    start=(g == 0 and nb % 2 == 0), stop=(g == 1 and nb % 2 == 1),
+                )
+
+        def finish_marks(hm):
+            sizes = [sb.tile([P, 2, HM], F32, tag="staged", bufs=4, name="size") for u in range(2)]
+            mark = sb.tile([P, N // P, HM], F32, tag="page0%d" % hm, align_bytes=64, name="mark")
+            for u in range(2):
+                nc.scalar.activation(out=sizes[u][:], in_=marks[hm][u][:], func=ACT.Abs)
+            for u in range(2):
+                nc.scalar.activation(out=mark[:, 2 * u : 2 * u + 2, :], in_=sizes[u][:], func=ACT.Exp, scale=-1.0)
+            nc.scalar.dma_start(out=out_0[:, HM * hm : HM * (hm + 1)].rearrange("(b p) m -> p b m", p=P), in_=mark[:])
+
+        for hm in range(2):
+            marks_pass(0, hm)
+
+        planes1 = [sb.tile([P, PACK, S], BF16, tag="FB"[half], align_bytes=64, name="planes1") for half in range(2)]
+        for t in range(4):
+            store_page(1, t)
+            cast_plane(1, t, planes1)
+        codes0 = sb.tile([P, T2], U32, align_bytes=64, name="codes0")
+
+        def finish_codes0(half):
+            quantise_page(0, half, grouped0[:, PACK * S * half : PACK * S * (half + 1)], codes0)
+            store_codes(0, slice(S * half, S * (half + 1)), codes0)
+
+        for half in range(2):
+            finish_codes0(half)
+        x1 = sb.tile([P, 2, PACK, HM], F32, tag="C", align_bytes=64, name="x1")
+        x1_grouped = sb.tile([P, PACK * M], BF16, tag="w4_words1", align_bytes=64, name="x1_grouped")
+        for hm in range(2):
+            slots = slice(HM * hm, HM * (hm + 1))
+            for t in range(4):
+                nc.vector.tensor_tensor(
+                    x1[:, hm, t, :], pages[1, t][:].indirect(entries(idx3, HM * hm, HM)), swell_rows[1][:, t, slots], ALU.add
+                )
+            part = x1_grouped[:, PACK * HM * hm : PACK * HM * (hm + 1)]
+            interleave(nc.vector.tensor_copy, part, x1[:, hm, :, :])
+            nc.vector.quantize_mx(out=x_mx[1][0][:, slots].bitcast(FP8X4), scales=x_mx[1][1][:, slots], in_=part)
+            marks_pass(1, hm)
+        grouped1 = sb.tile([P, PACK * T2], BF16, tag="h1", align_bytes=64, name="grouped1")
+        for c in range(4):
+            interleave(
+                nc.vector.tensor_copy if c == 3 else nc.scalar.copy,
+                grouped1[:, PACK * BANK * c : PACK * BANK * (c + 1)],
+                planes1[c // 2][:, :, BANK * (c % 2) : BANK * (c % 2 + 1)],
+            )
+            if c in (1, 2):
+                finish_marks(c - 1)
+        codes1 = sb.tile([P, T2], U32, tag="E", align_bytes=64, name="codes1")
+        for half in range(2):
+            quantise_page(1, half, grouped1[:, PACK * S * half : PACK * S * (half + 1)], codes1)
+            store_codes(1, slice(S * half, S * (half + 1)), codes1)
+        for q in range(4):
+            nc.sync.dma_start(
+                out=out_3[:, 4 * q : 4 * q + 4, :].rearrange("g r m -> r g m").bitcast(I32),
+                in_=page_scales[32 * q : 32 * q + 4, :, :].bitcast(I32),
+            )

@@ -56,7 +56,7 @@ def tile_list_heat_slot_marks_kernel(
                 in_=planes.rearrange("p t (c i) -> p c t i", i=4),
             )
 
-        def quantise_raw(raw, codes, scales, copy, tag="grouped", bufs=3):
+        def quantise_raw(raw, codes, scales, copy, tag="grouped", bufs=2):
             grouped = sb.tile([P, PACK * BANK], BF16, tag=tag, bufs=bufs, align_bytes=64, name="grouped")
             interleave(copy, grouped[:], raw[:])
             nc.vector.quantize_mx(out=codes[:].bitcast(FP8X4), scales=scales[:], in_=grouped[:])
@@ -92,11 +92,14 @@ def tile_list_heat_slot_marks_kernel(
             )
             return words
 
-        def load_gains(t):
-            gains = sb.tile([P, S], F32, tag="gains%d" % t, align_bytes=64, name="gains")
+        def load_gains(planes, cols, tag, queue=nc.sync):
+            tile = sb.tile([P, len(planes), len(cols)], F32, tag=tag, align_bytes=64, name="gains")
+            source = wgs.rearrange("(q t) j -> q t j", t=PACK)[:, planes.start : planes.stop, cols.start : cols.stop]
             for rep in (0, 2, 1, 3):
-                nc.sync.dma_start(out=gains[32 * rep : 32 * rep + 32, :], in_=wgs[t:P:PACK, :])
-            return gains
+                queue.dma_start(out=tile[32 * rep : 32 * rep + 32, :, :], in_=source)
+            for t in planes:
+                for j in range(cols.start, cols.stop, 256):
+                    gains[t, j] = (tile, t - planes.start, j - cols.start)
 
         idx = lists.tile([P, S // PER_COL], U16, name="idx")
         idx2 = lists.tile([P, S // PER_COL], U16, name="idx2")
@@ -114,18 +117,21 @@ def tile_list_heat_slot_marks_kernel(
 
         nc.sync.dma_start(idx[:], offs)
         table = [load_table(0)]
-        w1_raw = {(0, 0): load_raw(w1_source(0, 0), "E")}
         load_scale_rows(table_scales, tab_scales)
+        w1_raw = {(0, 0): load_raw(w1_source(0, 0), "E")}
         w4 = [load_w4(0)]
-        nc.sync.dma_start(idx2[:], offs2)
         w1_raw[1, 0] = load_raw(w1_source(1, 0), "F")
         table.append(load_table(1))
         load_scale_rows(w4_plane, w4_scales)
+        nc.sync.dma_start(idx2[:], offs2)
         pages = {}
-        gains = []
-        for t in range(3):
+        gains = {}
+        for t in range(2):
             pages[0, t] = load_page(0, t, "page0%d" % t)
-            gains.append(load_gains(t))
+        load_gains(range(0, 3), range(0, 256), "gains_a")
+        pages[0, 2] = load_page(0, 2, "page02")
+        load_gains(range(0, 3), range(256, 512), "gains_b")
+        load_gains(range(0, 3), range(512, S), "gains_c")
 
         clip_words = [sb.tile([P, S], U32, tag="CD"[a], align_bytes=64, name="clip_words") for a in range(2)]
         clip_scales = []
@@ -154,19 +160,17 @@ def tile_list_heat_slot_marks_kernel(
         quantise_w1(0, 0)
         gather_words(1, 0, S // 4)
         w1_mx[1, 0] = mx_tiles("w1_10")
-        grouped = sb.tile([P, PACK * BANK], BF16, tag="late_scales", align_bytes=64, name="grouped")
+        grouped = sb.tile([P, PACK * BANK], BF16, tag="grouped", bufs=2, align_bytes=64, name="grouped")
         for half, copy in enumerate((nc.scalar.copy, nc.vector.tensor_copy)):
             interleave(copy, grouped[:, 1024 * half : 1024 * (half + 1)], w1_raw[1, 0][:, :, 256 * half : 256 * (half + 1)])
         nc.vector.quantize_mx(out=w1_mx[1, 0][0][:].bitcast(FP8X4), scales=w1_mx[1, 0][1][:], in_=grouped[:])
         gather_words(1, S // 4, S // 4)
-        gather_scales("late_scales")
         gather_words(1, S // 2, S // 2)
 
         for a in range(2):
             w1_raw[a, 1] = load_raw(w1_source(a, 1), "EF"[a])
         w4.append(load_w4(1))
-        gains.append(load_gains(3))
-        nc.sync.dma_start(idx3[:], offs3)
+        load_gains(range(3, 4), range(0, S), "gains_d")
         swell_rows = {}
 
         def load_swell(g, tag):
@@ -191,7 +195,10 @@ def tile_list_heat_slot_marks_kernel(
                             out=bank[:], lhsT=clip_words[a][:, cols].bitcast(FP8X4), lhsT_scale=clip_scales[jb // 4][:, a, P * (jb % 4) : P * (jb % 4 + 1)],
                             rhs=rhs, rhs_scale=rhs_scale, start=(a == 0), stop=(a == 1),
                         )
-                    size = sb.tile([P, PACK, P], F32, tag="staged", bufs=4, name="size")
+                    if (g, jb, second) == (0, 0, 0):
+                        size = sb.tile([P, PACK, P], F32, tag="late_scales", align_bytes=64, name="size")
+                    else:
+                        size = sb.tile([P, PACK, P], F32, tag="staged", bufs=4, name="size")
                     nc.scalar.activation(out=size[:], in_=bank[:].rearrange("j (q t) -> j t q", t=PACK), func=ACT.Abs)
                     sizes.append(size)
                 if jb % 2 == 0:
@@ -204,12 +211,15 @@ def tile_list_heat_slot_marks_kernel(
                         )
                     if jb % 2 == 1 and t % 2 == 1:
                         nc.scalar.copy(out=h[:, t - 1 : t + 1, P * (jb - 1) : P * (jb + 1)], in_=turned[t // 2][:])
+                if (g, jb) == (0, 0):
+                    gather_scales("late_scales")
             return h
 
         def scatter(g, t, h, first, count):
+            tile, row, col = gains[t, first]
             nc.vector.tensor_tensor(
                 pages[g, t][:].indirect(entries(idx2, first, count)),
-                h[:, t, first : first + count], gains[t][:, first : first + count], ALU.mult,
+                h[:, t, first : first + count], tile[:, row, col : col + count], ALU.mult,
             )
 
         def fetch(g, t, x):
@@ -238,13 +248,15 @@ def tile_list_heat_slot_marks_kernel(
                 scatter(0, t, h0, 256 * q, 256)
         quantise_w1(0, 1)
         quantise_w1(1, 1)
-        pages[0, 3] = load_page(0, 3, "E")
-        load_swell(0, "F")
+        pages[0, 3] = load_page(0, 3, "page03")
+        nc.sync.dma_start(idx3[:], offs3)
+        load_swell(0, "A")
         pages[1, 0] = load_page(1, 0, "page10")
         pages[1, 1] = load_page(1, 1, "page11")
         pages[1, 2] = load_page(1, 2, "page12")
-        w2_raw = [load_raw(rows_by_four(w2, g), "AB"[g]) for g in range(2)]
         pages[1, 3] = load_page(1, 3, "page13")
+        w2_raw = [load_raw(rows_by_four(w2, g), "GH"[g]) for g in range(2)]
+        load_swell(1, "B")
         h1 = make_h(1)
         scatter(0, 3, h0, 0, S)
         x0 = sb.tile([P, PACK, M], F32, tag="h0", align_bytes=64, name="x0")
@@ -255,15 +267,18 @@ def tile_list_heat_slot_marks_kernel(
         x_mx = [mx_tiles("x_%d" % g) for g in range(2)]
         for g in range(2):
             quantise_raw(w2_raw[g], *w2_mx[g], nc.scalar.copy)
-        load_swell(1, "A")
-        stage0 = [sb.tile([P, PACK, S], BF16, tag="CD"[half], align_bytes=64, name="stage0") for half in range(2)]
+        stage0 = [sb.tile([P, PACK, S], BF16, tag="EF"[half], align_bytes=64, name="stage0") for half in range(2)]
         quantise_raw(x0, *x_mx[0], nc.scalar.copy, "ident", 1)
         for t in range(4):
             cast_plane(0, t, stage0)
-        scatter(1, 0, h1, 0, 512)
-        scatter(1, 0, h1, 512, 512)
-        for t in range(1, 4):
-            scatter(1, t, h1, 0, S)
+        for q in range(2):
+            for t in range(2):
+                scatter(1, t, h1, 256 * q, 256)
+        for t in range(2):
+            scatter(1, t, h1, 512, 512)
+        for first, count in ((0, 256), (256, 256), (512, 512)):
+            scatter(1, 2, h1, first, count)
+        scatter(1, 3, h1, 0, S)
         grouped0 = sb.tile([P, PACK * T2], BF16, tag="h0", align_bytes=64, name="grouped0")
         for half in range(2):
             interleave(nc.scalar.copy, grouped0[:, PACK * S * half : PACK * S * (half + 1)], stage0[half][:])
@@ -293,11 +308,11 @@ def tile_list_heat_slot_marks_kernel(
         for hm in range(2):
             marks_pass(0, hm)
 
-        planes1 = [sb.tile([P, PACK, S], BF16, tag="FB"[half], align_bytes=64, name="planes1") for half in range(2)]
+        planes1 = [sb.tile([P, PACK, S], BF16, tag="EF"[half], align_bytes=64, name="planes1") for half in range(2)]
         for t in range(4):
             store_page(1, t)
             cast_plane(1, t, planes1)
-        codes0 = sb.tile([P, T2], U32, align_bytes=64, name="codes0")
+        codes0 = sb.tile([P, T2], U32, tag="G", align_bytes=64, name="codes0")
 
         def finish_codes0(half):
             quantise_page(0, half, grouped0[:, PACK * S * half : PACK * S * (half + 1)], codes0)
@@ -326,7 +341,7 @@ def tile_list_heat_slot_marks_kernel(
             )
             if c in (1, 2):
                 finish_marks(c - 1)
-        codes1 = sb.tile([P, T2], U32, tag="E", align_bytes=64, name="codes1")
+        codes1 = sb.tile([P, T2], U32, tag="A", align_bytes=64, name="codes1")
         for half in range(2):
             quantise_page(1, half, grouped1[:, PACK * S * half : PACK * S * (half + 1)], codes1)
             store_codes(1, slice(S * half, S * (half + 1)), codes1)

@@ -92,19 +92,17 @@ def tile_list_heat_slot_marks_kernel(
             )
             return words
 
-        def load_gains(planes, cols, tag, queue=nc.sync):
-            tile = sb.tile([P, len(planes), len(cols)], F32, tag=tag, align_bytes=64, name="gains")
-            source = wgs.rearrange("(q t) j -> q t j", t=PACK)[:, planes.start : planes.stop, cols.start : cols.stop]
+        gains = sb.tile([P, PACK, S], F32, name="gains")
+
+        def load_gains(planes, cols):
+            source = wgs.rearrange("(q t) j -> q t j", t=PACK)[:, planes, cols]
             for rep in (0, 2, 1, 3):
-                queue.dma_start(out=tile[32 * rep : 32 * rep + 32, :, :], in_=source)
-            for t in planes:
-                for j in range(cols.start, cols.stop, 256):
-                    gains[t, j] = (tile, t - planes.start, j - cols.start)
+                nc.sync.dma_start(out=gains[32 * rep : 32 * rep + 32, planes, cols], in_=source)
 
         idx = lists.tile([P, S // PER_COL], U16, name="idx")
         idx2 = lists.tile([P, S // PER_COL], U16, name="idx2")
         idx3 = lists.tile([P, M // PER_COL], U16, name="idx3")
-        table_scales = sb.tile([P, 2, T], U8, align_bytes=64, name="table_scales")
+        table_scales = sb.tile([P, 2, T], U8, tag="scale_rows", align_bytes=64, name="table_scales")
         w4_plane = sb.tile([P, 2, H], U8, align_bytes=64, name="w4_plane")
         nc.gpsimd.memset(table_scales[:, 0, :].bitcast(I32), 0)
         nc.vector.memset(table_scales[:, 1, :].bitcast(I32), 0)
@@ -125,13 +123,12 @@ def tile_list_heat_slot_marks_kernel(
         load_scale_rows(w4_plane, w4_scales)
         nc.sync.dma_start(idx2[:], offs2)
         pages = {}
-        gains = {}
         for t in range(2):
             pages[0, t] = load_page(0, t, "page0%d" % t)
-        load_gains(range(0, 3), range(0, 256), "gains_a")
+        load_gains(slice(0, 3), slice(0, 256))
         pages[0, 2] = load_page(0, 2, "page02")
-        load_gains(range(0, 3), range(256, 512), "gains_b")
-        load_gains(range(0, 3), range(512, S), "gains_c")
+        load_gains(slice(0, 3), slice(256, 512))
+        load_gains(slice(0, 3), slice(512, S))
 
         clip_words = [sb.tile([P, S], U32, tag="CD"[a], align_bytes=64, name="clip_words") for a in range(2)]
         clip_scales = []
@@ -167,39 +164,52 @@ def tile_list_heat_slot_marks_kernel(
         gather_words(1, S // 4, S // 4)
         gather_words(1, S // 2, S // 2)
 
+        w2_raw = []
         for a in range(2):
-            w1_raw[a, 1] = load_raw(w1_source(a, 1), "EF"[a])
+            w1_raw[a, 1] = load_raw(w1_source(a, 1), "GF"[a])
+            w2_raw.append(load_raw(rows_by_four(w2, a), "BE"[a]))
         w4.append(load_w4(1))
-        load_gains(range(3, 4), range(0, S), "gains_d")
+        load_gains(slice(3, 4), slice(0, S))
         swell_rows = {}
 
         def load_swell(g, tag):
             swell_rows[g] = sb.tile([P, PACK, M], F32, tag=tag, align_bytes=64, name="swell_rows")
             nc.sync.dma_start(out=swell_rows[g][:], in_=rows_by_four(swell, g))
 
+        def readings(g, jb):
+            cols = slice(P * jb, P * (jb + 1))
+            banks = []
+            for second in range(2):
+                bank = ps.tile([P, BANK], F32, tag="mm", bufs=4, name="reading")
+                for a in range(2):
+                    if second:
+                        rhs = w4[g][:, a, :].bitcast(FP4X4)
+                        rhs_scale = w4_plane[:, a, PASS * g : PASS * (g + 1)]
+                    else:
+                        rhs = w1_mx[a, g][0][:].bitcast(FP8X4)
+                        rhs_scale = w1_mx[a, g][1][:]
+                    nc.tensor.matmul_mx(
+                        out=bank[:], lhsT=clip_words[a][:, cols].bitcast(FP8X4),
+                        lhsT_scale=clip_scales[jb // 4][:, a, P * (jb % 4) : P * (jb % 4 + 1)],
+                        rhs=rhs, rhs_scale=rhs_scale, start=(a == 0), stop=(a == 1),
+                    )
+                banks.append(bank)
+            return banks
+
         def make_h(g):
             h = sb.tile([P, PACK, S], F32, tag="h%d" % g, align_bytes=64, name="h")
+            ahead = readings(g, 0)
             for jb in range(S // P):
-                cols = slice(P * jb, P * (jb + 1))
+                banks = ahead
+                if jb + 1 < S // P:
+                    ahead = readings(g, jb + 1)
                 sizes = []
                 for second in range(2):
-                    bank = ps.tile([P, BANK], F32, tag="mm", bufs=4, name="reading")
-                    for a in range(2):
-                        if second:
-                            rhs = w4[g][:, a, :].bitcast(FP4X4)
-                            rhs_scale = w4_plane[:, a, PASS * g : PASS * (g + 1)]
-                        else:
-                            rhs = w1_mx[a, g][0][:].bitcast(FP8X4)
-                            rhs_scale = w1_mx[a, g][1][:]
-                        nc.tensor.matmul_mx(
-                            out=bank[:], lhsT=clip_words[a][:, cols].bitcast(FP8X4), lhsT_scale=clip_scales[jb // 4][:, a, P * (jb % 4) : P * (jb % 4 + 1)],
-                            rhs=rhs, rhs_scale=rhs_scale, start=(a == 0), stop=(a == 1),
-                        )
                     if (g, jb, second) == (0, 0, 0):
                         size = sb.tile([P, PACK, P], F32, tag="late_scales", align_bytes=64, name="size")
                     else:
                         size = sb.tile([P, PACK, P], F32, tag="staged", bufs=4, name="size")
-                    nc.scalar.activation(out=size[:], in_=bank[:].rearrange("j (q t) -> j t q", t=PACK), func=ACT.Abs)
+                    nc.scalar.activation(out=size[:], in_=banks[second][:].rearrange("j (q t) -> j t q", t=PACK), func=ACT.Abs)
                     sizes.append(size)
                 if jb % 2 == 0:
                     turned = [ps.tile([P, 2, 2 * P], F32, tag="turned", bufs=4, name="turned") for u in range(2)]
@@ -216,10 +226,9 @@ def tile_list_heat_slot_marks_kernel(
             return h
 
         def scatter(g, t, h, first, count):
-            tile, row, col = gains[t, first]
             nc.vector.tensor_tensor(
                 pages[g, t][:].indirect(entries(idx2, first, count)),
-                h[:, t, first : first + count], tile[:, row, col : col + count], ALU.mult,
+                h[:, t, first : first + count], gains[:, t, first : first + count], ALU.mult,
             )
 
         def fetch(g, t, x):
@@ -241,13 +250,15 @@ def tile_list_heat_slot_marks_kernel(
                 out=out_2[g].rearrange("p m t -> p (m t)").bitcast(I32)[:, cols], in_=codes[:, cols].bitcast(I32)
             )
 
-        page_scales = sb.tile([P, 2, T2], U8, align_bytes=64, name="page_scales")
         h0 = make_h(0)
         for q in range(4):
             for t in range(3):
                 scatter(0, t, h0, 256 * q, 256)
-        quantise_w1(0, 1)
-        quantise_w1(1, 1)
+        w2_mx = [mx_tiles("w2_%d" % g) for g in range(2)]
+        x_mx = [mx_tiles("x_%d" % g) for g in range(2)]
+        for a in range(2):
+            quantise_w1(a, 1)
+            quantise_raw(w2_raw[a], *w2_mx[a], nc.scalar.copy, "page1%d" % (2 + a), 1)
         pages[0, 3] = load_page(0, 3, "page03")
         nc.sync.dma_start(idx3[:], offs3)
         load_swell(0, "A")
@@ -255,30 +266,24 @@ def tile_list_heat_slot_marks_kernel(
         pages[1, 1] = load_page(1, 1, "page11")
         pages[1, 2] = load_page(1, 2, "page12")
         pages[1, 3] = load_page(1, 3, "page13")
-        w2_raw = [load_raw(rows_by_four(w2, g), "GH"[g]) for g in range(2)]
         load_swell(1, "B")
         h1 = make_h(1)
         scatter(0, 3, h0, 0, S)
         x0 = sb.tile([P, PACK, M], F32, tag="h0", align_bytes=64, name="x0")
         for t in range(4):
             fetch(0, t, x0)
-            store_page(0, t)
-        w2_mx = [mx_tiles("w2_%d" % g) for g in range(2)]
-        x_mx = [mx_tiles("x_%d" % g) for g in range(2)]
-        for g in range(2):
-            quantise_raw(w2_raw[g], *w2_mx[g], nc.scalar.copy)
-        stage0 = [sb.tile([P, PACK, S], BF16, tag="EF"[half], align_bytes=64, name="stage0") for half in range(2)]
-        quantise_raw(x0, *x_mx[0], nc.scalar.copy, "ident", 1)
+        stage0 = [sb.tile([P, PACK, S], F32, tag="FE"[half], align_bytes=64, name="stage0") for half in range(2)]
+        for half in range(2):
+            for t in range(4):
+                nc.scalar.dma_start(out=stage0[half][:, t, :], in_=pages[0, t][:, S * half : S * (half + 1)])
         for t in range(4):
-            cast_plane(0, t, stage0)
-        for q in range(2):
+            store_page(0, t)
+        quantise_raw(x0, *x_mx[0], nc.scalar.copy, "ident", 1)
+        for half in range(2):
             for t in range(2):
-                scatter(1, t, h1, 256 * q, 256)
-        for t in range(2):
-            scatter(1, t, h1, 512, 512)
-        for first, count in ((0, 256), (256, 256), (512, 512)):
-            scatter(1, 2, h1, first, count)
-        scatter(1, 3, h1, 0, S)
+                scatter(1, t, h1, 512 * half, 512)
+        for t in range(2, 4):
+            scatter(1, t, h1, 0, S)
         grouped0 = sb.tile([P, PACK * T2], BF16, tag="h0", align_bytes=64, name="grouped0")
         for half in range(2):
             interleave(nc.scalar.copy, grouped0[:, PACK * S * half : PACK * S * (half + 1)], stage0[half][:])
@@ -308,10 +313,11 @@ def tile_list_heat_slot_marks_kernel(
         for hm in range(2):
             marks_pass(0, hm)
 
-        planes1 = [sb.tile([P, PACK, S], BF16, tag="EF"[half], align_bytes=64, name="planes1") for half in range(2)]
+        planes1 = [sb.tile([P, PACK, S], BF16, tag="FE"[half], align_bytes=64, name="planes1") for half in range(2)]
         for t in range(4):
             store_page(1, t)
             cast_plane(1, t, planes1)
+        page_scales = sb.tile([P, 2, T2], U8, tag="scale_rows", align_bytes=64, name="page_scales")
         codes0 = sb.tile([P, T2], U32, tag="G", align_bytes=64, name="codes0")
 
         def finish_codes0(half):
@@ -321,7 +327,7 @@ def tile_list_heat_slot_marks_kernel(
         for half in range(2):
             finish_codes0(half)
         x1 = sb.tile([P, 2, PACK, HM], F32, tag="C", align_bytes=64, name="x1")
-        x1_grouped = sb.tile([P, PACK * M], BF16, tag="w4_words1", align_bytes=64, name="x1_grouped")
+        x1_grouped = sb.tile([P, PACK * M], BF16, tag="D", align_bytes=64, name="x1_grouped")
         for hm in range(2):
             slots = slice(HM * hm, HM * (hm + 1))
             for t in range(4):

@@ -44,10 +44,10 @@ def tile_list_heat_slot_marks_kernel(
             return matrix[PASS * g + t : PASS * (g + 1) : PACK, :]
 
         def load_scale_rows(plane, scales):
-            for q in range(4):
+            for r in range(4):
                 nc.sync.dma_start(
-                    out=plane[32 * q : 32 * q + 4, :, :].bitcast(I32),
-                    in_=scales[:, 4 * q : 4 * q + 4, :].rearrange("a r c -> r a c").bitcast(I32),
+                    out=plane[r:P:32, :, :].bitcast(I32),
+                    in_=scales[:, r:16:4, :].rearrange("a q c -> q a c").bitcast(I32),
                 )
 
         def interleave(copy, out, planes):
@@ -94,10 +94,22 @@ def tile_list_heat_slot_marks_kernel(
 
         gains = sb.tile([P, PACK, S], F32, name="gains")
 
-        def load_gains(planes, cols):
-            source = wgs.rearrange("(q t) j -> q t j", t=PACK)[:, planes, cols]
-            for rep in (0, 2, 1, 3):
-                nc.sync.dma_start(out=gains[32 * rep : 32 * rep + 32, planes, cols], in_=source)
+        def build_gains(rows):
+            turned = [ps.tile([P, 4, P], F32, tag="mm", bufs=4, name="gains_turned") for half in range(2)]
+            for jb in range(S // P):
+                nc.tensor.transpose(turned[jb // 4][:, jb % 4, :], rows[:, P * jb : P * (jb + 1)], ident[:])
+            for half in range(2):
+                spread = sb.tile([P, 4, PACK, P], F32, tag="page1%d" % half, align_bytes=64, name="spread")
+                for jb in range(4):
+                    nc.scalar.copy(
+                        out=spread[:, jb, :, :].rearrange("j t (rep q) -> j t rep q", rep=4),
+                        in_=turned[half][:, jb, :].rearrange("j (q t) -> j t q", t=PACK).unsqueeze(2).to_broadcast([P, PACK, 4, 32]),
+                    )
+                for t in range(PACK):
+                    back = ps.tile([P, 4, P], F32, tag="turned", bufs=4, name="gains_back")
+                    for jb in range(4):
+                        nc.tensor.transpose(back[:, jb, :], spread[:, jb, t, :], ident[:])
+                    nc.scalar.copy(out=gains[:, t, BANK * half : BANK * (half + 1)], in_=back[:].rearrange("p b j -> p (b j)"))
 
         idx = lists.tile([P, S // PER_COL], U16, name="idx")
         idx2 = lists.tile([P, S // PER_COL], U16, name="idx2")
@@ -114,6 +126,9 @@ def tile_list_heat_slot_marks_kernel(
         make_identity(nc, ident[:])
 
         nc.sync.dma_start(idx[:], offs)
+        gain_rows = sb.tile([P, S], F32, tag="page03", align_bytes=64, name="gain_rows")
+        nc.sync.dma_start(out=gain_rows[:], in_=wgs)
+        build_gains(gain_rows)
         table = [load_table(0)]
         load_scale_rows(table_scales, tab_scales)
         w1_raw = {(0, 0): load_raw(w1_source(0, 0), "E")}
@@ -123,12 +138,8 @@ def tile_list_heat_slot_marks_kernel(
         load_scale_rows(w4_plane, w4_scales)
         nc.sync.dma_start(idx2[:], offs2)
         pages = {}
-        for t in range(2):
+        for t in range(3):
             pages[0, t] = load_page(0, t, "page0%d" % t)
-        load_gains(slice(0, 3), slice(0, 256))
-        pages[0, 2] = load_page(0, 2, "page02")
-        load_gains(slice(0, 3), slice(256, 512))
-        load_gains(slice(0, 3), slice(512, S))
 
         clip_words = [sb.tile([P, S], U32, tag="CD"[a], align_bytes=64, name="clip_words") for a in range(2)]
         clip_scales = []
@@ -148,28 +159,22 @@ def tile_list_heat_slot_marks_kernel(
 
         w1_mx = {}
 
-        def quantise_w1(a, g, *slot):
+        def quantise_w1(a, g, copy):
             w1_mx[a, g] = mx_tiles("w1_%d%d" % (a, g))
-            quantise_raw(w1_raw[a, g], *w1_mx[a, g], nc.scalar.copy, *slot)
+            quantise_raw(w1_raw[a, g], *w1_mx[a, g], copy)
 
         gather_words(0, 0, S)
         gather_scales("early_scales")
-        quantise_w1(0, 0)
+        quantise_w1(0, 0, nc.vector.tensor_copy)
         gather_words(1, 0, S // 4)
-        w1_mx[1, 0] = mx_tiles("w1_10")
-        grouped = sb.tile([P, PACK * BANK], BF16, tag="grouped", bufs=2, align_bytes=64, name="grouped")
-        for half, copy in enumerate((nc.scalar.copy, nc.vector.tensor_copy)):
-            interleave(copy, grouped[:, 1024 * half : 1024 * (half + 1)], w1_raw[1, 0][:, :, 256 * half : 256 * (half + 1)])
-        nc.vector.quantize_mx(out=w1_mx[1, 0][0][:].bitcast(FP8X4), scales=w1_mx[1, 0][1][:], in_=grouped[:])
+        quantise_w1(1, 0, nc.vector.tensor_copy)
         gather_words(1, S // 4, S // 4)
         gather_words(1, S // 2, S // 2)
+        gather_scales("B")
 
-        w2_raw = []
         for a in range(2):
-            w1_raw[a, 1] = load_raw(w1_source(a, 1), "GF"[a])
-            w2_raw.append(load_raw(rows_by_four(w2, a), "BE"[a]))
+            w1_raw[a, 1] = load_raw(w1_source(a, 1), "H%d" % a)
         w4.append(load_w4(1))
-        load_gains(slice(3, 4), slice(0, S))
         swell_rows = {}
 
         def load_swell(g, tag):
@@ -201,14 +206,11 @@ def tile_list_heat_slot_marks_kernel(
             ahead = readings(g, 0)
             for jb in range(S // P):
                 banks = ahead
-                if jb + 1 < S // P:
+                if jb + 1 < S // P and (g, jb) != (0, 1):
                     ahead = readings(g, jb + 1)
                 sizes = []
                 for second in range(2):
-                    if (g, jb, second) == (0, 0, 0):
-                        size = sb.tile([P, PACK, P], F32, tag="late_scales", align_bytes=64, name="size")
-                    else:
-                        size = sb.tile([P, PACK, P], F32, tag="staged", bufs=4, name="size")
+                    size = sb.tile([P, PACK, P], F32, tag="staged", bufs=4, name="size")
                     nc.scalar.activation(out=size[:], in_=banks[second][:].rearrange("j (q t) -> j t q", t=PACK), func=ACT.Abs)
                     sizes.append(size)
                 if jb % 2 == 0:
@@ -221,8 +223,8 @@ def tile_list_heat_slot_marks_kernel(
                         )
                     if jb % 2 == 1 and t % 2 == 1:
                         nc.scalar.copy(out=h[:, t - 1 : t + 1, P * (jb - 1) : P * (jb + 1)], in_=turned[t // 2][:])
-                if (g, jb) == (0, 0):
-                    gather_scales("late_scales")
+                if (g, jb) == (0, 1):
+                    ahead = readings(g, jb + 1)
             return h
 
         def scatter(g, t, h, first, count):
@@ -257,28 +259,28 @@ def tile_list_heat_slot_marks_kernel(
         w2_mx = [mx_tiles("w2_%d" % g) for g in range(2)]
         x_mx = [mx_tiles("x_%d" % g) for g in range(2)]
         for a in range(2):
-            quantise_w1(a, 1)
-            quantise_raw(w2_raw[a], *w2_mx[a], nc.scalar.copy, "page1%d" % (2 + a), 1)
+            quantise_w1(a, 1, nc.scalar.copy)
         pages[0, 3] = load_page(0, 3, "page03")
         nc.sync.dma_start(idx3[:], offs3)
         load_swell(0, "A")
         pages[1, 0] = load_page(1, 0, "page10")
         pages[1, 1] = load_page(1, 1, "page11")
+        w2_raw = [load_raw(rows_by_four(w2, g), "H%d" % g) for g in range(2)]
         pages[1, 2] = load_page(1, 2, "page12")
         pages[1, 3] = load_page(1, 3, "page13")
-        load_swell(1, "B")
+        load_swell(1, "swell1")
         h1 = make_h(1)
         scatter(0, 3, h0, 0, S)
         x0 = sb.tile([P, PACK, M], F32, tag="h0", align_bytes=64, name="x0")
         for t in range(4):
             fetch(0, t, x0)
-        stage0 = [sb.tile([P, PACK, S], F32, tag="FE"[half], align_bytes=64, name="stage0") for half in range(2)]
-        for half in range(2):
-            for t in range(4):
-                nc.scalar.dma_start(out=stage0[half][:, t, :], in_=pages[0, t][:, S * half : S * (half + 1)])
-        for t in range(4):
             store_page(0, t)
+        for g in range(2):
+            quantise_raw(w2_raw[g], *w2_mx[g], nc.scalar.copy)
+        stage0 = [sb.tile([P, PACK, S], BF16, tag="EF"[half], align_bytes=64, name="stage0") for half in range(2)]
         quantise_raw(x0, *x_mx[0], nc.scalar.copy, "ident", 1)
+        for t in range(4):
+            cast_plane(0, t, stage0)
         for half in range(2):
             for t in range(2):
                 scatter(1, t, h1, 512 * half, 512)
@@ -313,12 +315,17 @@ def tile_list_heat_slot_marks_kernel(
         for hm in range(2):
             marks_pass(0, hm)
 
-        planes1 = [sb.tile([P, PACK, S], BF16, tag="FE"[half], align_bytes=64, name="planes1") for half in range(2)]
+        planes1 = [sb.tile([P, PACK, S], BF16, tag="EF"[half], align_bytes=64, name="planes1") for half in range(2)]
         for t in range(4):
             store_page(1, t)
-            cast_plane(1, t, planes1)
+            for half in range(2 if t < 3 else 1):
+                nc.scalar.copy(out=planes1[half][:, t, :], in_=pages[1, t][:, S * half : S * (half + 1)])
         page_scales = sb.tile([P, 2, T2], U8, tag="scale_rows", align_bytes=64, name="page_scales")
-        codes0 = sb.tile([P, T2], U32, tag="G", align_bytes=64, name="codes0")
+        codes0 = sb.tile([P, T2], U32, tag="H0", align_bytes=64, name="codes0")
+
+        def store_scale_rows(g):
+            for r in range(4):
+                nc.sync.dma_start(out=out_3[g, r:16:4, :].bitcast(I32), in_=page_scales[r:P:32, g, :].bitcast(I32))
 
         def finish_codes0(half):
             quantise_page(0, half, grouped0[:, PACK * S * half : PACK * S * (half + 1)], codes0)
@@ -326,7 +333,8 @@ def tile_list_heat_slot_marks_kernel(
 
         for half in range(2):
             finish_codes0(half)
-        x1 = sb.tile([P, 2, PACK, HM], F32, tag="C", align_bytes=64, name="x1")
+        store_scale_rows(0)
+        x1 = sb.tile([P, 2, PACK, HM], F32, tag="h0", align_bytes=64, name="x1")
         x1_grouped = sb.tile([P, PACK * M], BF16, tag="D", align_bytes=64, name="x1_grouped")
         for hm in range(2):
             slots = slice(HM * hm, HM * (hm + 1))
@@ -339,20 +347,15 @@ def tile_list_heat_slot_marks_kernel(
             nc.vector.quantize_mx(out=x_mx[1][0][:, slots].bitcast(FP8X4), scales=x_mx[1][1][:, slots], in_=part)
             marks_pass(1, hm)
         grouped1 = sb.tile([P, PACK * T2], BF16, tag="h1", align_bytes=64, name="grouped1")
-        for c in range(4):
-            interleave(
-                nc.vector.tensor_copy if c == 3 else nc.scalar.copy,
-                grouped1[:, PACK * BANK * c : PACK * BANK * (c + 1)],
-                planes1[c // 2][:, :, BANK * (c % 2) : BANK * (c % 2 + 1)],
-            )
-            if c in (1, 2):
-                finish_marks(c - 1)
         codes1 = sb.tile([P, T2], U32, tag="A", align_bytes=64, name="codes1")
-        for half in range(2):
+        for half, copy in enumerate((nc.scalar.copy, nc.vector.tensor_copy)):
+            for c in range(2):
+                part = grouped1[:, PACK * (S * half + BANK * c) : PACK * (S * half + BANK * (c + 1))]
+                interleave(copy, part, planes1[half][:, :, BANK * c : BANK * (c + 1)])
             quantise_page(1, half, grouped1[:, PACK * S * half : PACK * S * (half + 1)], codes1)
             store_codes(1, slice(S * half, S * (half + 1)), codes1)
-        for q in range(4):
-            nc.sync.dma_start(
-                out=out_3[:, 4 * q : 4 * q + 4, :].rearrange("g r m -> r g m").bitcast(I32),
-                in_=page_scales[32 * q : 32 * q + 4, :, :].bitcast(I32),
-            )
+            if half == 0:
+                nc.scalar.copy(out=planes1[1][:, 3, :], in_=pages[1, 3][:, S:T2])
+        for hm in range(2):
+            finish_marks(hm)
+        store_scale_rows(1)

from contextlib import ExitStack

import concourse.mybir as mybir
from concourse.masks import make_identity

K, T, S, H, T2, M, N = 1024, 2048, 1024, 1024, 2048, 512, 512
FLOPS = 2 * (2 * K * H * S + H * N * M)

F32 = mybir.dt.float32
BF16 = mybir.dt.bfloat16
I32 = mybir.dt.int32
U32 = mybir.dt.uint32
U16 = mybir.dt.uint16
U8 = mybir.dt.uint8
FP8X4 = mybir.dt.float8_e4m3fn_x4
FP4X4 = mybir.dt.float4_e2m1fn_x4
ALU = mybir.AluOpType
ACT = mybir.ActivationFunctionType

P = 128
PACK = 4
PASS = P * PACK
BANK = 512
PER_COL = 16


def tile_list_heat_slot_marks_kernel(
    tc, tab_words, tab_scales, offs, offs2, offs3, w1, w4_words, w4_scales, wgs, page0, swell, w2,
    out_0, out_1, out_2, out_3,
):
    nc = tc.nc
    with ExitStack() as ctx:
        lists = ctx.enter_context(tc.tile_pool(name="lists", bufs=1))
        sb = ctx.enter_context(tc.tile_pool(name="sb", bufs=1))
        ps = ctx.enter_context(tc.psum_pool(name="ps", bufs=1))

        def entries(tile, first, count):
            return tile[:, first // PER_COL : (first + count) // PER_COL]

        def rows_by_four(matrix, g):
            return matrix[PASS * g : PASS * (g + 1), :].rearrange("(p t) c -> p t c", t=PACK)

        def page_rows(matrix, g, t):
            return matrix[PASS * g + t : PASS * (g + 1) : PACK, :]

        def load_scale_rows(plane, scales):
            for r in range(4):
                nc.sync.dma_start(
                    out=plane[r:P:32, :, :].bitcast(I32),
                    in_=scales[:, r:16:4, :].rearrange("a q c -> q a c").bitcast(I32),
                )

        def interleave(copy, out, planes):
            copy(
                out=out.rearrange("p (c i t) -> p c t i", i=4, t=PACK),
                in_=planes.rearrange("p t (c i) -> p c t i", i=4),
            )

        def quantise_raw(raw, codes, scales, copy, tag="grouped", bufs=2):
            grouped = sb.tile([P, PACK * BANK], BF16, tag=tag, bufs=bufs, align_bytes=64, name="grouped")
            interleave(copy, grouped[:], raw[:])
            nc.vector.quantize_mx(out=codes[:].bitcast(FP8X4), scales=scales[:], in_=grouped[:])

        def load_raw(source, tag):
            raw = sb.tile([P, PACK, BANK], F32, tag=tag, align_bytes=64, name="raw")
            nc.sync.dma_start(out=raw[:], in_=source)
            return raw

        def mx_tiles(name):
            codes = sb.tile([P, BANK], U32, align_bytes=64, name=name + "_codes")
            scales = sb.tile([P, BANK], U8, align_bytes=64, name=name + "_scales")
            return codes, scales

        def w1_source(a, g):
            return w1[PASS * a : PASS * (a + 1), PASS * g : PASS * (g + 1)].rearrange("(p i) c -> p i c", i=PACK)

        def load_page(g, t, tag, queue=nc.sync):
            page = sb.tile([P, T2], F32, tag=tag, align_bytes=64, name="page")
            queue.dma_start(out=page[:], in_=page_rows(page0, g, t))
            return page

        def load_table(a):
            words = sb.tile([P, T], I32, tag="AB"[a], align_bytes=64, name="table")
            nc.sync.dma_start(out=words[:], in_=tab_words[a].rearrange("p t i -> p (t i)").bitcast(I32))
            return words

        def load_w4(g):
            words = sb.tile([P, 2, 2 * PASS], U8, align_bytes=64, tag="w4_words%d" % g, bufs=1, name="w4_words")
            nc.sync.dma_start(
                out=words[:].bitcast(I32),
                in_=w4_words[:, :, 2 * PASS * g : 2 * PASS * (g + 1)].rearrange("a p c -> p a c").bitcast(I32),
            )
            return words

        gains = sb.tile([P, PACK, S], F32, name="gains")

        def build_gains(rows):
            turned = [ps.tile([P, 4, P], F32, tag="mm", bufs=4, name="gains_turned") for half in range(2)]
            for jb in range(S // P):
                nc.tensor.transpose(turned[jb // 4][:, jb % 4, :], rows[:, P * jb : P * (jb + 1)], ident[:])
            for half in range(2):
                spread = sb.tile([P, 4, PACK, P], F32, tag="page1%d" % half, align_bytes=64, name="spread")
                for jb in range(4):
                    nc.scalar.copy(
                        out=spread[:, jb, :, :].rearrange("j t (rep q) -> j t rep q", rep=4),
                        in_=turned[half][:, jb, :].rearrange("j (q t) -> j t q", t=PACK).unsqueeze(2).to_broadcast([P, PACK, 4, 32]),
                    )
                for t in range(PACK):
                    back = ps.tile([P, 4, P], F32, tag="turned", bufs=4, name="gains_back")
                    for jb in range(4):
                        nc.tensor.transpose(back[:, jb, :], spread[:, jb, t, :], ident[:])
                    nc.scalar.copy(out=gains[:, t, BANK * half : BANK * (half + 1)], in_=back[:].rearrange("p b j -> p (b j)"))

        idx = lists.tile([P, S // PER_COL], U16, name="idx")
        idx2 = lists.tile([P, S // PER_COL], U16, name="idx2")
        idx3 = lists.tile([P, M // PER_COL], U16, name="idx3")
        table_scales = sb.tile([P, 2, T], U8, tag="scale_rows", align_bytes=64, name="table_scales")
        w4_plane = sb.tile([P, 2, H], U8, align_bytes=64, name="w4_plane")
        nc.gpsimd.memset(table_scales[:, 0, :].bitcast(I32), 0)
        nc.vector.memset(table_scales[:, 1, :].bitcast(I32), 0)
        nc.vector.memset(w4_plane[:].rearrange("p a c -> p (a c)").bitcast(I32), 0)
        warm = sb.tile([P, 2], F32, name="warm")
        nc.vector.memset(warm[:, 0:1], 0.0)
        nc.scalar.activation(out=warm[:, 1:2], in_=warm[:, 0:1], func=ACT.Exp)
        ident = sb.tile([P, P], F32, tag="ident", align_bytes=64, name="ident")
        make_identity(nc, ident[:])

        nc.sync.dma_start(idx[:], offs)
        gain_rows = sb.tile([P, S], F32, tag="page03", align_bytes=64, name="gain_rows")
        nc.sync.dma_start(out=gain_rows[:], in_=wgs)
        build_gains(gain_rows)
        table = [load_table(0)]
        load_scale_rows(table_scales, tab_scales)
        w1_raw = {(0, 0): load_raw(w1_source(0, 0), "E")}
        w4 = [load_w4(0)]
        w1_raw[1, 0] = load_raw(w1_source(1, 0), "F")
        table.append(load_table(1))
        load_scale_rows(w4_plane, w4_scales)
        nc.sync.dma_start(idx2[:], offs2)
        pages = {}
        for t in range(3):
            pages[0, t] = load_page(0, t, "page0%d" % t)

        clip_words = [sb.tile([P, S], U32, tag="CD"[a], align_bytes=64, name="clip_words") for a in range(2)]
        clip_scales = []

        def gather_scales(tag):
            first = len(clip_scales) * BANK
            picked = sb.tile([P, 2, BANK], U8, tag=tag, align_bytes=64, name="clip_scales")
            for a in range(2):
                nc.vector.tensor_copy(picked[:, a, :], table_scales[:, a, :].indirect(entries(idx, first, BANK)))
            clip_scales.append(picked)

        def gather_words(a, first, count):
            nc.vector.tensor_copy(
                clip_words[a][:, first : first + count],
                table[a][:].bitcast(U32).indirect(entries(idx, first, count)),
            )

        w1_mx = {}

        def quantise_w1(a, g, copy):
            w1_mx[a, g] = mx_tiles("w1_%d%d" % (a, g))
            quantise_raw(w1_raw[a, g], *w1_mx[a, g], copy)

        gather_words(0, 0, S)
        gather_scales("early_scales")
        quantise_w1(0, 0, nc.vector.tensor_copy)
        gather_words(1, 0, S // 4)
        quantise_w1(1, 0, nc.vector.tensor_copy)
        gather_words(1, S // 4, S // 4)
        gather_words(1, S // 2, S // 2)
        gather_scales("B")

        for a in range(2):
            w1_raw[a, 1] = load_raw(w1_source(a, 1), "H%d" % a)
        w4.append(load_w4(1))
        swell_rows = {}

        def load_swell(g, tag):
            swell_rows[g] = sb.tile([P, PACK, M], F32, tag=tag, align_bytes=64, name="swell_rows")
            nc.sync.dma_start(out=swell_rows[g][:], in_=rows_by_four(swell, g))

        def readings(g, jb):
            cols = slice(P * jb, P * (jb + 1))
            banks = []
            for second in range(2):
                bank = ps.tile([P, BANK], F32, tag="mm", bufs=4, name="reading")
                for a in range(2):
                    if second:
                        rhs = w4[g][:, a, :].bitcast(FP4X4)
                        rhs_scale = w4_plane[:, a, PASS * g : PASS * (g + 1)]
                    else:
                        rhs = w1_mx[a, g][0][:].bitcast(FP8X4)
                        rhs_scale = w1_mx[a, g][1][:]
                    nc.tensor.matmul_mx(
                        out=bank[:], lhsT=clip_words[a][:, cols].bitcast(FP8X4),
                        lhsT_scale=clip_scales[jb // 4][:, a, P * (jb % 4) : P * (jb % 4 + 1)],
                        rhs=rhs, rhs_scale=rhs_scale, start=(a == 0), stop=(a == 1),
                    )
                banks.append(bank)
            return banks

        def make_h(g):
            h = sb.tile([P, PACK, S], F32, tag="h%d" % g, align_bytes=64, name="h")
            ahead = readings(g, 0)
            for jb in range(S // P):
                banks = ahead
                if jb + 1 < S // P and (g, jb) != (0, 1):
                    ahead = readings(g, jb + 1)
                sizes = []
                for second in range(2):
                    size = sb.tile([P, PACK, P], F32, tag="staged", bufs=4, name="size")
                    nc.scalar.activation(out=size[:], in_=banks[second][:].rearrange("j (q t) -> j t q", t=PACK), func=ACT.Abs)
                    sizes.append(size)
                if jb % 2 == 0:
                    turned = [ps.tile([P, 2, 2 * P], F32, tag="turned", bufs=4, name="turned") for u in range(2)]
                for t in range(PACK):
                    for second in (1, 0):
                        nc.tensor.matmul(
                            out=turned[t // 2][:, t % 2, P * (jb % 2) : P * (jb % 2 + 1)], lhsT=sizes[second][:, t, :], rhs=ident[:],
                            start=(second == 1), stop=(second == 0), is_transpose=True,
                        )
                    if jb % 2 == 1 and t % 2 == 1:
                        nc.scalar.copy(out=h[:, t - 1 : t + 1, P * (jb - 1) : P * (jb + 1)], in_=turned[t // 2][:])
                if (g, jb) == (0, 1):
                    ahead = readings(g, jb + 1)
            return h

        def scatter(g, t, h, first, count):
            nc.vector.tensor_tensor(
                pages[g, t][:].indirect(entries(idx2, first, count)),
                h[:, t, first : first + count], gains[:, t, first : first + count], ALU.mult,
            )

        def fetch(g, t, x):
            nc.vector.tensor_tensor(x[:, t, :], pages[g, t][:].indirect(idx3[:]), swell_rows[g][:, t, :], ALU.add)

        def store_page(g, t):
            nc.sync.dma_start(out=page_rows(out_1, g, t), in_=pages[g, t][:])

        def cast_plane(g, t, planes):
            for half in range(2):
                nc.scalar.copy(out=planes[half][:, t, :], in_=pages[g, t][:, S * half : S * (half + 1)])

        def quantise_page(g, half, grouped, codes):
            cols = slice(S * half, S * (half + 1))
            nc.vector.quantize_mx(out=codes[:, cols].bitcast(FP8X4), scales=page_scales[:, g, cols], in_=grouped)

        def store_codes(g, cols, codes):
            nc.sync.dma_start(
                out=out_2[g].rearrange("p m t -> p (m t)").bitcast(I32)[:, cols], in_=codes[:, cols].bitcast(I32)
            )

        h0 = make_h(0)
        for q in range(4):
            for t in range(3):
                scatter(0, t, h0, 256 * q, 256)
        w2_mx = [mx_tiles("w2_%d" % g) for g in range(2)]
        x_mx = [mx_tiles("x_%d" % g) for g in range(2)]
        for a in range(2):
            quantise_w1(a, 1, nc.scalar.copy)
        pages[0, 3] = load_page(0, 3, "page03")
        nc.sync.dma_start(idx3[:], offs3)
        load_swell(0, "A")
        pages[1, 0] = load_page(1, 0, "page10")
        pages[1, 1] = load_page(1, 1, "page11")
        w2_raw = [load_raw(rows_by_four(w2, g), "H%d" % g) for g in range(2)]
        pages[1, 2] = load_page(1, 2, "page12")
        pages[1, 3] = load_page(1, 3, "page13")
        load_swell(1, "swell1")
        h1 = make_h(1)
        scatter(0, 3, h0, 0, S)
        x0 = sb.tile([P, PACK, M], F32, tag="h0", align_bytes=64, name="x0")
        for t in range(4):
            fetch(0, t, x0)
            store_page(0, t)
        for g in range(2):
            quantise_raw(w2_raw[g], *w2_mx[g], nc.scalar.copy)
        stage0 = [sb.tile([P, PACK, S], BF16, tag="EF"[half], align_bytes=64, name="stage0") for half in range(2)]
        quantise_raw(x0, *x_mx[0], nc.scalar.copy, "ident", 1)
        for t in range(4):
            cast_plane(0, t, stage0)
        for half in range(2):
            for t in range(2):
                scatter(1, t, h1, 512 * half, 512)
        for t in range(2, 4):
            scatter(1, t, h1, 0, S)
        grouped0 = sb.tile([P, PACK * T2], BF16, tag="h0", align_bytes=64, name="grouped0")
        for half in range(2):
            interleave(nc.scalar.copy, grouped0[:, PACK * S * half : PACK * S * (half + 1)], stage0[half][:])

        HM = M // 2
        marks = [[ps.tile([P, 2, HM], F32, tag="mm", bufs=4, name="marks") for u in range(2)] for hm in range(2)]

        def marks_pass(g, hm):
            for nb in range(N // P):
                cols = slice(P * nb, P * (nb + 1))
                slots = slice(HM * hm, HM * (hm + 1))
                nc.tensor.matmul_mx(
                    out=marks[hm][nb // 2][:, nb % 2, :], lhsT=w2_mx[g][0][:, cols].bitcast(FP8X4), lhsT_scale=w2_mx[g][1][:, cols],
                    rhs=x_mx[g][0][:, slots].bitcast(FP8X4), rhs_scale=x_mx[g][1][:, slots],
                    start=(g == 0 and nb % 2 == 0), stop=(g == 1 and nb % 2 == 1),
                )

        def finish_marks(hm):
            sizes = [sb.tile([P, 2, HM], F32, tag="staged", bufs=4, name="size") for u in range(2)]
            mark = sb.tile([P, N // P, HM], F32, tag="page0%d" % hm, align_bytes=64, name="mark")
            for u in range(2):
                nc.scalar.activation(out=sizes[u][:], in_=marks[hm][u][:], func=ACT.Abs)
            for u in range(2):
                nc.scalar.activation(out=mark[:, 2 * u : 2 * u + 2, :], in_=sizes[u][:], func=ACT.Exp, scale=-1.0)
            nc.scalar.dma_start(out=out_0[:, HM * hm : HM * (hm + 1)].rearrange("(b p) m -> p b m", p=P), in_=mark[:])

        for hm in range(2):
            marks_pass(0, hm)

        planes1 = [sb.tile([P, PACK, S], BF16, tag="EF"[half], align_bytes=64, name="planes1") for half in range(2)]
        for t in range(4):
            store_page(1, t)
            for half in range(2 if t < 3 else 1):
                nc.scalar.copy(out=planes1[half][:, t, :], in_=pages[1, t][:, S * half : S * (half + 1)])
        page_scales = sb.tile([P, 2, T2], U8, tag="scale_rows", align_bytes=64, name="page_scales")
        codes0 = sb.tile([P, T2], U32, tag="H0", align_bytes=64, name="codes0")

        def store_scale_rows(g):
            for r in range(4):
                nc.sync.dma_start(out=out_3[g, r:16:4, :].bitcast(I32), in_=page_scales[r:P:32, g, :].bitcast(I32))

        def finish_codes0(half):
            quantise_page(0, half, grouped0[:, PACK * S * half : PACK * S * (half + 1)], codes0)
            store_codes(0, slice(S * half, S * (half + 1)), codes0)

        for half in range(2):
            finish_codes0(half)
        store_scale_rows(0)
        x1 = sb.tile([P, 2, PACK, HM], F32, tag="h0", align_bytes=64, name="x1")
        x1_grouped = sb.tile([P, PACK * M], BF16, tag="D", align_bytes=64, name="x1_grouped")
        for hm in range(2):
            slots = slice(HM * hm, HM * (hm + 1))
            for t in range(4):
                nc.vector.tensor_tensor(
                    x1[:, hm, t, :], pages[1, t][:].indirect(entries(idx3, HM * hm, HM)), swell_rows[1][:, t, slots], ALU.add
                )
            part = x1_grouped[:, PACK * HM * hm : PACK * HM * (hm + 1)]
            interleave(nc.vector.tensor_copy, part, x1[:, hm, :, :])
            nc.vector.quantize_mx(out=x_mx[1][0][:, slots].bitcast(FP8X4), scales=x_mx[1][1][:, slots], in_=part)
            marks_pass(1, hm)
        grouped1 = sb.tile([P, PACK * T2], BF16, tag="h1", align_bytes=64, name="grouped1")
        codes1 = sb.tile([P, T2], U32, tag="A", align_bytes=64, name="codes1")
        for half, copy in enumerate((nc.scalar.copy, nc.vector.tensor_copy)):
            for c in range(2):
                part = grouped1[:, PACK * (S * half + BANK * c) : PACK * (S * half + BANK * (c + 1))]
                interleave(copy, part, planes1[half][:, :, BANK * c : BANK * (c + 1)])
            quantise_page(1, half, grouped1[:, PACK * S * half : PACK * S * (half + 1)], codes1)
            store_codes(1, slice(S * half, S * (half + 1)), codes1)
            if half == 0:
                nc.scalar.copy(out=planes1[1][:, 3, :], in_=pages[1, 3][:, S:T2])
        for hm in range(2):
            finish_marks(hm)
        store_scale_rows(1)
